import numpy as np
import ml_dtypes


def mxq(x, axis, fmt="e4m3"):
    dtype, down = {"e4m3": (ml_dtypes.float8_e4m3fn, 7), "e5m2": (ml_dtypes.float8_e5m2, 14)}[fmt]
    v = np.moveaxis(np.asarray(x, np.float32).astype(ml_dtypes.bfloat16).astype(np.float64), axis, -1)
    blocks = v.reshape(v.shape[:-1] + (-1, 32))
    amax = np.abs(blocks).max(-1, keepdims=True)
    byte = np.maximum(np.where(amax > 0, np.frexp(amax)[1] - 1 + 127, 0) - down, 1)
    scale = np.exp2(byte - 127.0)
    codes = (blocks / scale).astype(np.float32).astype(dtype).astype(np.float64)
    return np.moveaxis((codes * scale).reshape(v.shape), -1, axis)


WIDE = False


def mx_kscale(k):
    if not WIDE:
        return np.ones(k)
    levels = np.array([10, -10, 5, -5, 0])
    if k % 512:
        return np.exp2(np.random.permutation(np.resize(levels, k // 32))).repeat(32)
    a = np.empty((k // 512, 16))
    for p in range(k // 512):
        a[p, :8] = np.random.permutation(np.resize(levels, 8))
        for g in range(8):
            far = levels[np.abs(levels - a[p, g]) >= 10]
            a[p, g + 8] = far[np.random.randint(len(far))]
    return np.exp2(a.ravel()).repeat(32)


def f64(x):
    return np.asarray(x).astype(np.float64)


def striped(idx):
    return np.tile(idx.reshape(-1, 16).T, (8, 1)).astype(np.uint16)


def unstriped(offs):
    return offs[:16].T.reshape(-1).astype(np.int64)


def striped8(idx):
    return np.concatenate([x.reshape(-1, 16).T for x in idx]).astype(np.uint16)


def runs(offs, k):
    lists = np.stack([offs[16 * r : 16 * r + 16].T.reshape(-1) for r in range(8)]).astype(np.int64)
    return lists[np.arange(k) % 512 // 64]


def pack_weight(w):
    k, n = w.shape
    w = f64(np.asarray(w, np.float32).astype(ml_dtypes.bfloat16)).reshape(k // 32, 32, n)
    amax = np.abs(w).max(1)
    byte = np.clip(np.where(amax > 0, np.frexp(amax)[1] - 1 + 127 - 7, 1), 1, 254)
    scaled = (w * np.exp2(127.0 - byte)[:, None, :]).reshape(k, n).astype(np.float32)
    words = np.ascontiguousarray(scaled.reshape(k // 512, 128, 4, n).transpose(0, 1, 3, 2)).astype(ml_dtypes.float8_e4m3fn).view(np.uint8)
    return words, np.ascontiguousarray(byte.astype(np.uint8).reshape(k // 512, 16, n))


def unpack_weight(words, scales):
    g, p, n, _ = words.shape
    vals = np.ascontiguousarray(words).view(ml_dtypes.float8_e4m3fn).astype(np.float64) * np.repeat(np.exp2(scales.astype(np.float64) - 127.0), 8, axis=1)[..., None]
    return vals.transpose(0, 1, 3, 2).reshape(g * 512, n)


def sigmoid(v):
    return 1.0 / (1.0 + np.exp(-np.maximum(v, -700.0)))

def planes(y):
    n, m = y.shape
    v = y.astype(np.float32).astype(ml_dtypes.bfloat16).astype(np.float64).reshape(n // 32, 32, m)
    top = np.abs(v).max(1)
    byte = np.clip(np.where(top > 0, np.frexp(top)[1] - 1 + 127 - 7, 1), 1, 254)
    codes = (v * np.exp2(127.0 - byte)[:, None, :]).reshape(n, m).astype(np.float32).astype(ml_dtypes.float8_e4m3fn).view(np.uint8)
    words = codes.reshape(n // 512, 128, 4, m).transpose(0, 1, 3, 2)
    return np.ascontiguousarray(words), np.ascontiguousarray(byte.astype(np.uint8).reshape(n // 512, 16, m))


K, T, S, N, H = 512, 2048, 512, 512, 512


def setup_inputs():
    n = np.random.standard_normal
    s = mx_kscale(K)[:, None]
    u = mx_kscale(H)
    packed_xT = pack_weight(n((K, T)) * s)
    packed_w1 = pack_weight(n((K, H)) / np.sqrt(K) / s)
    packed_w2 = pack_weight(n((H, N)) / np.sqrt(H) / u[:, None])
    return {
        "x_words": packed_xT[0],
        "x_scales": packed_xT[1],
        "w1_words": packed_w1[0],
        "w1_scales": packed_w1[1],
        "gn": (np.random.uniform(0.5, 1.5, (H, 1)) * u[:, None]).astype(np.float32),
        "w2_words": packed_w2[0],
        "w2_scales": packed_w2[1],
        "offs": striped(np.random.permutation(T)[:S]),
        "n1": striped8(np.stack([np.random.permutation(S) for _ in range(8)])),
        "n2": striped8(np.stack([np.random.permutation(S) for _ in range(8)])),
        "n3": striped8(np.stack([np.random.permutation(S) for _ in range(8)])),
        "n4": striped8(np.stack([np.random.permutation(S) for _ in range(8)])),
    }


def reference(x_words, x_scales, w1_words, w1_scales, gn, w2_words, w2_scales, offs, n1, n2, n3, n4):
    xq = unpack_weight(x_words, x_scales)[:, unstriped(offs)]
    y = unpack_weight(w1_words, w1_scales).T @ xq
    z = f64(gn) * ((y - (y[np.arange(H)[:, None], runs(n1, H)])) / (np.abs(y[np.arange(H)[:, None], runs(n2, H)] - y) + 0.5))
    h = unpack_weight(w2_words, w2_scales).T @ mxq(z, 0, "e4m3")
    out_0 = h + (sigmoid(y[np.arange(H)[:, None], runs(n4, H)] - y)) * (h[np.arange(N)[:, None], runs(n3, N)] - h)
    return (out_0,) + planes(out_0)

@@ -1,0 +1,223 @@
+from contextlib import ExitStack
+
+import concourse.mybir as mybir
+
+K, T, S, N, H = 512, 2048, 512, 512, 512
+FLOPS = 2 * K * H * S + 2 * H * N * S
+
+F32 = mybir.dt.float32
+BF16 = mybir.dt.bfloat16
+I32 = mybir.dt.int32
+U32 = mybir.dt.uint32
+U16 = mybir.dt.uint16
+U8 = mybir.dt.uint8
+FP8X4 = mybir.dt.float8_e4m3fn_x4
+ALU = mybir.AluOpType
+ACT = mybir.ActivationFunctionType
+
+P = 128
+PACK = 4
+HALF = S // 2
+TINY = 2.0 ** -60
+
+
+def load_scale_rows(engine, plane, scales, quadrants=range(4)):
+    for q in quadrants:
+        engine.dma_start(out=plane[32 * q : 32 * q + 4, :].bitcast(I32), in_=scales[0, 4 * q : 4 * q + 4, :].bitcast(I32))
+
+
+def packed_rows(words):
+    return words[0].rearrange("p n t -> p (n t)").bitcast(I32)
+
+
+def tile_picked_skippullbfrac_none_po_kernel(
+    tc, x_words, x_scales, w1_words, w1_scales, gn, w2_words, w2_scales, offs, n1, n2, n3, n4, out_0, out_1, out_2
+):
+    nc = tc.nc
+    with ExitStack() as ctx:
+        lists = ctx.enter_context(tc.tile_pool(name="lists", bufs=1))
+        keep = ctx.enter_context(tc.tile_pool(name="keep", bufs=1))
+        psum = ctx.enter_context(tc.psum_pool(name="psum", bufs=1))
+
+        def sb(name, shape, dtype, tag=None):
+            return keep.tile(shape, dtype, name=name, tag=tag or name, align_bytes=64)
+
+        offs_sb = lists.tile([P, S // 16], U16, name="offs_sb")
+        n1_sb = lists.tile([P, S // 16], U16, name="n1_sb")
+        n2_sb = lists.tile([P, S // 16], U16, name="n2_sb")
+        n3_sb = lists.tile([P, S // 16], U16, name="n3_sb")
+        n4_sb = lists.tile([P, S // 16], U16, name="n4_sb")
+
+        x_codes = sb("x_codes", [P, T], U32)
+        x_plane = sb("x_plane", [P, T], U8)
+        w1_codes_raw = sb("w1_codes_raw", [P, H], I32)
+        w1_plane_raw = sb("w1_plane_raw", [P, H], U8)
+        w2_codes_raw = sb("w2_codes_raw", [P, N], I32)
+        w2_plane_raw = sb("w2_plane_raw", [P, N], U8)
+        gain = sb("gain", [P, PACK], F32)
+        tiny = sb("tiny", [P, 1], F32)
+        warm = sb("warm", [P, 1], F32)
+
+        nc.gpsimd.memset(w1_plane_raw[:].bitcast(I32), 0)
+        nc.gpsimd.memset(x_plane[:].bitcast(I32), 0)
+        nc.vector.memset(w2_plane_raw[:].bitcast(I32), 0)
+        nc.vector.memset(tiny[:], TINY)
+        nc.scalar.activation(warm[:], tiny[:], ACT.Ln)
+
+        nc.sync.dma_start(offs_sb[:], offs)
+        nc.sync.dma_start(out=x_codes[:].bitcast(I32), in_=packed_rows(x_words))
+        load_scale_rows(nc.sync, x_plane, x_scales)
+        nc.sync.dma_start(out=w1_codes_raw[:], in_=packed_rows(w1_words))
+        load_scale_rows(nc.sync, w1_plane_raw, w1_scales, range(0, 2))
+        load_scale_rows(nc.gpsimd, w1_plane_raw, w1_scales, range(2, 4))
+        nc.sync.dma_start(n2_sb[:], n2)
+        nc.sync.dma_start(n1_sb[:], n1)
+        nc.sync.dma_start(n4_sb[:], n4)
+        nc.sync.dma_start(out=w2_codes_raw[:], in_=packed_rows(w2_words))
+        load_scale_rows(nc.sync, w2_plane_raw, w2_scales)
+        nc.sync.dma_start(out=gain[:], in_=gn.rearrange("(p t) o -> p (t o)", t=PACK))
+        nc.sync.dma_start(n3_sb[:], n3)
+
+        y_win = [sb("y_win%d" % t, [P, 2 * S], F32) for t in range(PACK)]
+        for t in range(PACK):
+            nc.vector.memset(y_win[t][:, S:], 0.0)
+
+        def deal(name, codes_raw, plane_raw):
+            codes = sb(name + "_codes", [P, PACK, P], I32)
+            plane = sb(name + "_plane", [P, PACK, P], U8)
+            nc.vector.tensor_copy(out=codes[:], in_=codes_raw[:].rearrange("p (m t) -> p t m", t=PACK))
+            nc.vector.tensor_copy(out=plane[:], in_=plane_raw[:].rearrange("p (m t) -> p t m", t=PACK))
+            return codes, plane
+
+        xq_plane = sb("xq_plane", [P, S], U8)
+        xq_codes = sb("xq_codes", [P, S], U32)
+        nc.vector.tensor_copy(xq_plane[:], x_plane[:].indirect(offs_sb[:]))
+        nc.vector.tensor_copy(xq_codes[:], x_codes[:].indirect(offs_sb[:]))
+        w1_codes, w1_plane = deal("w1", w1_codes_raw, w1_plane_raw)
+
+        y_ps = [psum.tile([P, S], F32, name="y_ps%d" % t) for t in range(PACK)]
+        h_ps = [psum.tile([P, S], F32, name="h_ps%d" % t) for t in range(PACK)]
+        y_flat = sb("y_flat", [P, PACK, S], F32)
+        for t in range(PACK):
+            nc.tensor.matmul_mx(
+                out=y_ps[t][:],
+                lhsT=w1_codes[:, t, :].bitcast(FP8X4),
+                lhsT_scale=w1_plane[:, t, :],
+                rhs=xq_codes[:].bitcast(FP8X4),
+                rhs_scale=xq_plane[:],
+                start=True,
+                stop=True,
+            )
+            nc.scalar.copy(y_win[t][:, :S], y_ps[t][:])
+            nc.scalar.copy(y_flat[:, t, :], y_ps[t][:])
+
+        w2_codes, w2_plane = deal("w2", w2_codes_raw, w2_plane_raw)
+        gain2 = sb("gain2", [P, PACK], F32)
+        nc.vector.tensor_scalar(gain2[:], gain[:], -2.0, None, ALU.mult)
+
+        d1 = sb("d1", [P, PACK, S], F32)
+        d2 = sb("d2", [P, PACK, S], F32)
+        d4_early = sb("d4_early", [P, 2, S], F32)
+        mag = sb("mag", [P, PACK, S], F32)
+        logs = sb("logs", [P, PACK, S], F32)
+
+        def diff(dst, t, places):
+            nc.vector.tensor_tensor(dst, y_win[t][:].indirect(places[:]), y_flat[:, t, :], ALU.subtract)
+
+        for t in range(PACK):
+            diff(d2[:, t, :], t, n2_sb)
+            nc.scalar.activation(mag[:, t, :], d2[:, t, :], ACT.Abs)
+            nc.scalar.activation(logs[:, t, :], mag[:, t, :], ACT.Ln, bias=tiny[:], scale=2.0)
+        for t in range(PACK):
+            diff(d1[:, t, :], t, n1_sb)
+        for t in range(2):
+            diff(d4_early[:, t, :], t, n4_sb)
+
+        recip = mag[:].rearrange("p c (t i) -> p t c i", t=PACK)
+        z_planes = sb("z_planes", [P, PACK, S], BF16)
+        for t in range(PACK):
+            nc.scalar.activation(recip[:, t], logs[:, t, :].rearrange("p (c i) -> p c i", c=PACK), ACT.Sigmoid, scale=-1.0)
+            nc.vector.scalar_tensor_tensor(
+                z_planes[:, t, :].rearrange("p (c i) -> p c i", c=PACK),
+                d1[:, t, :].rearrange("p (c i) -> p c i", c=PACK),
+                gain2[:, t : t + 1],
+                recip[:, t],
+                ALU.mult,
+                ALU.mult,
+            )
+        gate = logs
+        for t in range(2):
+            nc.scalar.activation(gate[:, t, :], d4_early[:, t, :], ACT.Sigmoid)
+
+        z_grouped = sb("z_grouped", [P, S, PACK], BF16, tag="z_grouped")
+        nc.scalar.copy(z_grouped[:, :HALF, :], z_planes[:, :, :HALF].rearrange("p t j -> p j t"))
+        nc.vector.tensor_copy(z_grouped[:, HALF:, :], z_planes[:, :, HALF:].rearrange("p t j -> p j t"))
+        z_codes = sb("z_codes", [P, S], U32)
+        z_plane = sb("z_plane", [P, S], U8)
+        nc.vector.quantize_mx(out=z_codes[:].bitcast(FP8X4), scales=z_plane[:], in_=z_grouped[:].rearrange("p j t -> p (j t)"))
+
+        h_win = [sb("h_win%d" % t, [P, S], F32) for t in range(PACK)]
+        for t in range(PACK):
+            nc.tensor.matmul_mx(
+                out=h_ps[t][:],
+                lhsT=w2_codes[:, t, :].bitcast(FP8X4),
+                lhsT_scale=w2_plane[:, t, :],
+                rhs=z_codes[:].bitcast(FP8X4),
+                rhs_scale=z_plane[:],
+                start=True,
+                stop=True,
+            )
+            nc.scalar.copy(h_win[t][:], h_ps[t][:])
+
+        d4_late = sb("d4_late", [P, 2, S], F32, tag="z_grouped")
+        for t in range(2, PACK):
+            diff(d4_late[:, t - 2, :], t, n4_sb)
+            nc.scalar.activation(gate[:, t, :], d4_late[:, t - 2, :], ACT.Sigmoid)
+
+        pulled = sb("pulled", [P, PACK, S], F32)
+        kept = sb("kept", [P, PACK, S], F32)
+        res = sb("res", [P, PACK, S], F32)
+        res_grouped = sb("res_grouped", [P, S, PACK], BF16)
+        res_codes = sb("res_codes", [P, S], U32)
+        res_plane = sb("res_plane", [P, S], U8)
+        out_rows = out_0.rearrange("(p t) j -> p t j", t=PACK)
+        out_words = packed_rows(out_1)
+
+        def mix(t, cols):
+            places = n3_sb[:, cols.start // 16 : cols.stop // 16]
+            nc.vector.tensor_tensor(pulled[:, t, cols], h_win[t][:].indirect(places), gate[:, t, cols], ALU.mult)
+            nc.vector.scalar_tensor_tensor(kept[:, t, cols], gate[:, t, cols], 1.0, h_ps[t][:, cols], ALU.subtract, ALU.mult)
+
+        def finish(t, cols):
+            nc.vector.tensor_tensor(res[:, t, cols], pulled[:, t, cols], kept[:, t, cols], ALU.subtract)
+
+        def regroup(copy, cols):
+            copy(res_grouped[:, cols, :], res[:, :, cols].rearrange("p t j -> p j t"))
+
+        def hand_on(cols):
+            nc.vector.quantize_mx(
+                out=res_codes[:, cols].bitcast(FP8X4),
+                scales=res_plane[:, cols],
+                in_=res_grouped[:, cols, :].rearrange("p j t -> p (j t)"),
+            )
+            nc.sync.dma_start(out=out_words[:, cols], in_=res_codes[:, cols].bitcast(I32))
+
+        first, second = slice(0, HALF), slice(HALF, S)
+        steps = [(t, cols) for cols in (first, second) for t in range(PACK)]
+        for i, step in enumerate(steps):
+            mix(*step)
+            if i > 0:
+                finish(*steps[i - 1])
+            if i == PACK:
+                nc.sync.dma_start(out=out_rows[:, :, first], in_=res[:, :, first])
+                regroup(nc.scalar.copy, first)
+            if i == PACK + 2:
+                hand_on(first)
+        finish(*steps[-1])
+        nc.sync.dma_start(out=out_rows[:, :, second], in_=res[:, :, second])
+        regroup(nc.scalar.copy, slice(HALF, HALF + 64))
+        regroup(nc.vector.tensor_copy, slice(HALF + 64, S))
+        hand_on(second)
+        for q in range(4):
+            engine = nc.sync if q % 2 == 0 else nc.scalar
+            engine.dma_start(out=out_2[0, 4 * q : 4 * q + 4, :].bitcast(I32), in_=res_plane[32 * q : 32 * q + 4, :].bitcast(I32))

@@ -18,6 +18,8 @@ ACT = mybir.ActivationFunctionType
 P = 128
 PACK = 4
 HALF = S // 2
+HALVES = (slice(0, HALF), slice(HALF, S))
+WHOLE = slice(0, S)
 TINY = 2.0 ** -60
 
 
@@ -28,6 +30,10 @@ def load_scale_rows(engine, plane, scales, quadrants=range(4)):
 
 def packed_rows(words):
     return words[0].rearrange("p n t -> p (n t)").bitcast(I32)
+
+
+def entries(places, cols):
+    return places[:, cols.start // 16 : cols.stop // 16]
 
 
 def tile_picked_skippullbfrac_none_po_kernel(
@@ -41,6 +47,20 @@ def tile_picked_skippullbfrac_none_po_kernel(
 
         def sb(name, shape, dtype, tag=None):
             return keep.tile(shape, dtype, name=name, tag=tag or name, align_bytes=64)
+
+        def bank(name, number, width):
+            return psum.tile([P, width], F32, name=name, tag="bank%d" % number)
+
+        def product(out, codes, plane, t, rhs_codes, rhs_plane):
+            nc.tensor.matmul_mx(
+                out=out,
+                lhsT=codes[:, t, :].bitcast(FP8X4),
+                lhsT_scale=plane[:, t, :],
+                rhs=rhs_codes.bitcast(FP8X4),
+                rhs_scale=rhs_plane,
+                start=True,
+                stop=True,
+            )
 
         offs_sb = lists.tile([P, S // 16], U16, name="offs_sb")
         n1_sb = lists.tile([P, S // 16], U16, name="n1_sb")
@@ -59,70 +79,67 @@ def tile_picked_skippullbfrac_none_po_kernel(
         warm = sb("warm", [P, 1], F32)
 
         nc.gpsimd.memset(w1_plane_raw[:].bitcast(I32), 0)
-        nc.gpsimd.memset(x_plane[:].bitcast(I32), 0)
-        nc.vector.memset(w2_plane_raw[:].bitcast(I32), 0)
+        nc.vector.memset(x_plane[:].bitcast(I32), 0)
         nc.vector.memset(tiny[:], TINY)
+        nc.vector.memset(w2_plane_raw[:].bitcast(I32), 0)
         nc.scalar.activation(warm[:], tiny[:], ACT.Ln)
 
         nc.sync.dma_start(offs_sb[:], offs)
-        nc.sync.dma_start(out=x_codes[:].bitcast(I32), in_=packed_rows(x_words))
+        nc.sync.dma_start(out=x_codes[:, : T // 2].bitcast(I32), in_=packed_rows(x_words)[:, : T // 2])
         load_scale_rows(nc.sync, x_plane, x_scales)
+        nc.sync.dma_start(out=x_codes[:, T // 2 :].bitcast(I32), in_=packed_rows(x_words)[:, T // 2 :])
         nc.sync.dma_start(out=w1_codes_raw[:], in_=packed_rows(w1_words))
         load_scale_rows(nc.sync, w1_plane_raw, w1_scales, range(0, 2))
         load_scale_rows(nc.gpsimd, w1_plane_raw, w1_scales, range(2, 4))
         nc.sync.dma_start(n2_sb[:], n2)
-        nc.sync.dma_start(n1_sb[:], n1)
-        nc.sync.dma_start(n4_sb[:], n4)
         nc.sync.dma_start(out=w2_codes_raw[:], in_=packed_rows(w2_words))
         load_scale_rows(nc.sync, w2_plane_raw, w2_scales)
+        nc.sync.dma_start(n1_sb[:], n1)
+        nc.sync.dma_start(n4_sb[:], n4)
         nc.sync.dma_start(out=gain[:], in_=gn.rearrange("(p t) o -> p (t o)", t=PACK))
         nc.sync.dma_start(n3_sb[:], n3)
 
-        y_win = [sb("y_win%d" % t, [P, 2 * S], F32) for t in range(PACK)]
-        for t in range(PACK):
-            nc.vector.memset(y_win[t][:, S:], 0.0)
+        def deal_codes(name, raw):
+            codes = sb(name, [P, PACK, P], I32)
+            nc.vector.tensor_copy(out=codes[:], in_=raw[:].rearrange("p (m t) -> p t m", t=PACK))
+            return codes
 
-        def deal(name, codes_raw, plane_raw):
-            codes = sb(name + "_codes", [P, PACK, P], I32)
-            plane = sb(name + "_plane", [P, PACK, P], U8)
-            nc.vector.tensor_copy(out=codes[:], in_=codes_raw[:].rearrange("p (m t) -> p t m", t=PACK))
-            nc.vector.tensor_copy(out=plane[:], in_=plane_raw[:].rearrange("p (m t) -> p t m", t=PACK))
-            return codes, plane
+        def deal_plane(name, raw):
+            plane = sb(name, [P, PACK, P], U8)
+            nc.vector.tensor_copy(out=plane[:], in_=raw[:].rearrange("p (m t) -> p t m", t=PACK))
+            return plane
 
         xq_plane = sb("xq_plane", [P, S], U8)
         xq_codes = sb("xq_codes", [P, S], U32)
         nc.vector.tensor_copy(xq_plane[:], x_plane[:].indirect(offs_sb[:]))
-        nc.vector.tensor_copy(xq_codes[:], x_codes[:].indirect(offs_sb[:]))
-        w1_codes, w1_plane = deal("w1", w1_codes_raw, w1_plane_raw)
+        w1_plane = deal_plane("w1_plane", w1_plane_raw)
+        nc.vector.tensor_copy(xq_codes[:, HALVES[0]], x_codes[:].indirect(entries(offs_sb, HALVES[0])))
+        w1_codes = deal_codes("w1_codes", w1_codes_raw)
+        nc.vector.tensor_copy(xq_codes[:, HALVES[1]], x_codes[:].indirect(entries(offs_sb, HALVES[1])))
 
-        y_ps = [psum.tile([P, S], F32, name="y_ps%d" % t) for t in range(PACK)]
-        h_ps = [psum.tile([P, S], F32, name="h_ps%d" % t) for t in range(PACK)]
-        y_flat = sb("y_flat", [P, PACK, S], F32)
-        for t in range(PACK):
-            nc.tensor.matmul_mx(
-                out=y_ps[t][:],
-                lhsT=w1_codes[:, t, :].bitcast(FP8X4),
-                lhsT_scale=w1_plane[:, t, :],
-                rhs=xq_codes[:].bitcast(FP8X4),
-                rhs_scale=xq_plane[:],
-                start=True,
-                stop=True,
-            )
-            nc.scalar.copy(y_win[t][:, :S], y_ps[t][:])
-            nc.scalar.copy(y_flat[:, t, :], y_ps[t][:])
+        y_win = [sb("y_win%d" % t, [P, S if t == 0 else 2 * S], F32) for t in range(PACK)]
+        y_last = sb("y_last", [P, S], F32)
+        y_flat = [y_win[t + 1][:, S:] for t in range(PACK - 1)] + [y_last[:]]
+        y_pieces = [(0, HALVES[0]), (0, HALVES[1])] + [(t, WHOLE) for t in range(1, PACK)]
+        for number, (t, cols) in enumerate(y_pieces):
+            y_ps = bank("y_ps%d" % number, number, cols.stop - cols.start)
+            product(y_ps[:], w1_codes, w1_plane, t, xq_codes[:, cols], xq_plane[:, cols])
+            nc.scalar.copy(y_win[t][:, cols], y_ps[:])
+            nc.scalar.copy(y_flat[t][:, cols], y_ps[:])
 
-        w2_codes, w2_plane = deal("w2", w2_codes_raw, w2_plane_raw)
+        w2_codes = deal_codes("w2_codes", w2_codes_raw)
+        w2_plane = deal_plane("w2_plane", w2_plane_raw)
         gain2 = sb("gain2", [P, PACK], F32)
         nc.vector.tensor_scalar(gain2[:], gain[:], -2.0, None, ALU.mult)
 
         d1 = sb("d1", [P, PACK, S], F32)
         d2 = sb("d2", [P, PACK, S], F32)
-        d4_early = sb("d4_early", [P, 2, S], F32)
         mag = sb("mag", [P, PACK, S], F32)
         logs = sb("logs", [P, PACK, S], F32)
 
         def diff(dst, t, places):
-            nc.vector.tensor_tensor(dst, y_win[t][:].indirect(places[:]), y_flat[:, t, :], ALU.subtract)
+            for cols in HALVES if t == 0 else (WHOLE,):
+                nc.vector.tensor_tensor(dst[:, cols], y_win[t][:].indirect(entries(places, cols)), y_flat[t][:, cols], ALU.subtract)
 
         for t in range(PACK):
             diff(d2[:, t, :], t, n2_sb)
@@ -130,49 +147,53 @@ def tile_picked_skippullbfrac_none_po_kernel(
             nc.scalar.activation(logs[:, t, :], mag[:, t, :], ACT.Ln, bias=tiny[:], scale=2.0)
         for t in range(PACK):
             diff(d1[:, t, :], t, n1_sb)
-        for t in range(2):
-            diff(d4_early[:, t, :], t, n4_sb)
+        d4_first = sb("d4_first", [P, S], F32)
+        diff(d4_first[:], 0, n4_sb)
 
-        recip = mag[:].rearrange("p c (t i) -> p t c i", t=PACK)
+        recip = mag[:].rearrange("p c (u t i) -> p u t c i", u=2, t=PACK)
         z_planes = sb("z_planes", [P, PACK, S], BF16)
-        for t in range(PACK):
-            nc.scalar.activation(recip[:, t], logs[:, t, :].rearrange("p (c i) -> p c i", c=PACK), ACT.Sigmoid, scale=-1.0)
-            nc.vector.scalar_tensor_tensor(
-                z_planes[:, t, :].rearrange("p (c i) -> p c i", c=PACK),
-                d1[:, t, :].rearrange("p (c i) -> p c i", c=PACK),
-                gain2[:, t : t + 1],
-                recip[:, t],
-                ALU.mult,
-                ALU.mult,
-            )
-        gate = logs
-        for t in range(2):
-            nc.scalar.activation(gate[:, t, :], d4_early[:, t, :], ACT.Sigmoid)
-
-        z_grouped = sb("z_grouped", [P, S, PACK], BF16, tag="z_grouped")
-        nc.scalar.copy(z_grouped[:, :HALF, :], z_planes[:, :, :HALF].rearrange("p t j -> p j t"))
-        nc.vector.tensor_copy(z_grouped[:, HALF:, :], z_planes[:, :, HALF:].rearrange("p t j -> p j t"))
+        z_grouped = [sb("z_grouped%d" % u, [P, HALF, PACK], BF16) for u in range(2)]
         z_codes = sb("z_codes", [P, S], U32)
         z_plane = sb("z_plane", [P, S], U8)
-        nc.vector.quantize_mx(out=z_codes[:].bitcast(FP8X4), scales=z_plane[:], in_=z_grouped[:].rearrange("p j t -> p (j t)"))
-
+        for u, cols in enumerate(HALVES):
+            for t in range(PACK):
+                nc.scalar.activation(recip[:, u, t], logs[:, t, cols].rearrange("p (c i) -> p c i", c=PACK), ACT.Sigmoid, scale=-1.0)
+                nc.vector.scalar_tensor_tensor(
+                    z_planes[:, t, cols].rearrange("p (c i) -> p c i", c=PACK),
+                    d1[:, t, cols].rearrange("p (c i) -> p c i", c=PACK),
+                    gain2[:, t : t + 1],
+                    recip[:, u, t],
+                    ALU.mult,
+                    ALU.mult,
+                )
+        gate = logs
         h_win = [sb("h_win%d" % t, [P, S], F32) for t in range(PACK)]
-        for t in range(PACK):
-            nc.tensor.matmul_mx(
-                out=h_ps[t][:],
-                lhsT=w2_codes[:, t, :].bitcast(FP8X4),
-                lhsT_scale=w2_plane[:, t, :],
-                rhs=z_codes[:].bitcast(FP8X4),
-                rhs_scale=z_plane[:],
-                start=True,
-                stop=True,
-            )
-            nc.scalar.copy(h_win[t][:], h_ps[t][:])
+        h_ps = {}
 
-        d4_late = sb("d4_late", [P, 2, S], F32, tag="z_grouped")
-        for t in range(2, PACK):
-            diff(d4_late[:, t - 2, :], t, n4_sb)
-            nc.scalar.activation(gate[:, t, :], d4_late[:, t - 2, :], ACT.Sigmoid)
+        def gate_of(t, d4):
+            nc.scalar.activation(gate[:, t, :], d4, ACT.Sigmoid)
+
+        def second_layer(u, cols):
+            nc.vector.quantize_mx(
+                out=z_codes[:, cols].bitcast(FP8X4), scales=z_plane[:, cols], in_=z_grouped[u][:].rearrange("p j t -> p (j t)")
+            )
+            for pair in range(2):
+                h_ps[pair, u] = bank("h_ps%d_%d" % (pair, u), PACK + 2 * u + pair, S)
+                for e in range(2):
+                    product(h_ps[pair, u][:, HALVES[e]], w2_codes, w2_plane, 2 * pair + e, z_codes[:, cols], z_plane[:, cols])
+
+        for u, cols in enumerate(HALVES):
+            nc.scalar.copy(z_grouped[u][:], z_planes[:, :, cols].rearrange("p t j -> p j t"))
+        second_layer(0, HALVES[0])
+        diff(d1[:, 3, :], 1, n4_sb)
+        second_layer(1, HALVES[1])
+        diff(d1[:, 2, :], 2, n4_sb)
+        diff(d1[:, 1, :], 3, n4_sb)
+        d4 = [d4_first[:], d1[:, 3, :], d1[:, 2, :], d1[:, 1, :]]
+        for t in range(PACK):
+            gate_of(t, d4[t])
+            for u, cols in enumerate(HALVES):
+                nc.scalar.copy(h_win[t][:, cols], h_ps[t // 2, u][:, HALVES[t % 2]])
 
         pulled = sb("pulled", [P, PACK, S], F32)
         kept = sb("kept", [P, PACK, S], F32)
@@ -183,13 +204,19 @@ def tile_picked_skippullbfrac_none_po_kernel(
         out_rows = out_0.rearrange("(p t) j -> p t j", t=PACK)
         out_words = packed_rows(out_1)
 
-        def mix(t, cols):
-            places = n3_sb[:, cols.start // 16 : cols.stop // 16]
-            nc.vector.tensor_tensor(pulled[:, t, cols], h_win[t][:].indirect(places), gate[:, t, cols], ALU.mult)
-            nc.vector.scalar_tensor_tensor(kept[:, t, cols], gate[:, t, cols], 1.0, h_ps[t][:, cols], ALU.subtract, ALU.mult)
+        def pull(t, cols):
+            nc.vector.tensor_tensor(pulled[:, t, cols], h_win[t][:].indirect(entries(n3_sb, cols)), gate[:, t, cols], ALU.mult)
 
-        def finish(t, cols):
-            nc.vector.tensor_tensor(res[:, t, cols], pulled[:, t, cols], kept[:, t, cols], ALU.subtract)
+        def keep_own(pair, u):
+            rows = slice(2 * pair, 2 * pair + 2)
+            h_pair = h_ps[pair, u][:].rearrange("p (e j) -> p e j", e=2)
+            nc.vector.scalar_tensor_tensor(
+                kept[:, rows, HALVES[u]], gate[:, rows, HALVES[u]], 1.0, h_pair, ALU.subtract, ALU.mult
+            )
+
+        def finish(cols):
+            nc.vector.tensor_tensor(res[:, :, cols], pulled[:, :, cols], kept[:, :, cols], ALU.subtract)
+            nc.sync.dma_start(out=out_rows[:, :, cols], in_=res[:, :, cols])
 
         def regroup(copy, cols):
             copy(res_grouped[:, cols, :], res[:, :, cols].rearrange("p t j -> p j t"))
@@ -202,22 +229,26 @@ def tile_picked_skippullbfrac_none_po_kernel(
             )
             nc.sync.dma_start(out=out_words[:, cols], in_=res_codes[:, cols].bitcast(I32))
 
-        first, second = slice(0, HALF), slice(HALF, S)
-        steps = [(t, cols) for cols in (first, second) for t in range(PACK)]
-        for i, step in enumerate(steps):
-            mix(*step)
-            if i > 0:
-                finish(*steps[i - 1])
-            if i == PACK:
-                nc.sync.dma_start(out=out_rows[:, :, first], in_=res[:, :, first])
-                regroup(nc.scalar.copy, first)
-            if i == PACK + 2:
-                hand_on(first)
-        finish(*steps[-1])
-        nc.sync.dma_start(out=out_rows[:, :, second], in_=res[:, :, second])
-        regroup(nc.scalar.copy, slice(HALF, HALF + 64))
-        regroup(nc.vector.tensor_copy, slice(HALF + 64, S))
-        hand_on(second)
+        pieces = (slice(0, HALF), slice(HALF, HALF + 128), slice(HALF + 128, S))
+        for t in range(PACK):
+            if t % 2 == 0:
+                keep_own(t // 2, 0)
+            pull(t, pieces[0])
+        keep_own(0, 1)
+        finish(pieces[0])
+        regroup(nc.scalar.copy, pieces[0])
+        keep_own(1, 1)
+        for t in range(PACK):
+            pull(t, pieces[1])
+        hand_on(pieces[0])
+        finish(pieces[1])
+        regroup(nc.scalar.copy, pieces[1])
+        for t in range(PACK):
+            pull(t, pieces[2])
+        hand_on(pieces[1])
+        finish(pieces[2])
+        regroup(nc.vector.tensor_copy, pieces[2])
+        hand_on(pieces[2])
         for q in range(4):
             engine = nc.sync if q % 2 == 0 else nc.scalar
             engine.dma_start(out=out_2[0, 4 * q : 4 * q + 4, :].bitcast(I32), in_=res_plane[32 * q : 32 * q + 4, :].bitcast(I32))

@@ -87,10 +87,10 @@ def tile_picked_skippullbfrac_none_po_kernel(
         nc.sync.dma_start(offs_sb[:], offs)
         nc.sync.dma_start(out=x_codes[:, : T // 2].bitcast(I32), in_=packed_rows(x_words)[:, : T // 2])
         load_scale_rows(nc.sync, x_plane, x_scales)
-        nc.sync.dma_start(out=x_codes[:, T // 2 :].bitcast(I32), in_=packed_rows(x_words)[:, T // 2 :])
         nc.sync.dma_start(out=w1_codes_raw[:], in_=packed_rows(w1_words))
-        load_scale_rows(nc.sync, w1_plane_raw, w1_scales, range(0, 2))
-        load_scale_rows(nc.gpsimd, w1_plane_raw, w1_scales, range(2, 4))
+        nc.sync.dma_start(out=x_codes[:, T // 2 :].bitcast(I32), in_=packed_rows(x_words)[:, T // 2 :])
+        load_scale_rows(nc.sync, w1_plane_raw, w1_scales, range(0, 1))
+        load_scale_rows(nc.gpsimd, w1_plane_raw, w1_scales, range(1, 4))
         nc.sync.dma_start(n2_sb[:], n2)
         nc.sync.dma_start(out=w2_codes_raw[:], in_=packed_rows(w2_words))
         load_scale_rows(nc.sync, w2_plane_raw, w2_scales)
@@ -104,18 +104,19 @@ def tile_picked_skippullbfrac_none_po_kernel(
             nc.vector.tensor_copy(out=codes[:], in_=raw[:].rearrange("p (m t) -> p t m", t=PACK))
             return codes
 
-        def deal_plane(name, raw):
+        def deal_plane(name, raw, steps):
             plane = sb(name, [P, PACK, P], U8)
-            nc.vector.tensor_copy(out=plane[:], in_=raw[:].rearrange("p (m t) -> p t m", t=PACK))
+            for rows in steps:
+                nc.vector.tensor_copy(out=plane[:, rows, :], in_=raw[:].rearrange("p (m t) -> p t m", t=PACK)[:, rows, :])
             return plane
 
         xq_plane = sb("xq_plane", [P, S], U8)
         xq_codes = sb("xq_codes", [P, S], U32)
         nc.vector.tensor_copy(xq_plane[:], x_plane[:].indirect(offs_sb[:]))
-        w1_plane = deal_plane("w1_plane", w1_plane_raw)
-        nc.vector.tensor_copy(xq_codes[:, HALVES[0]], x_codes[:].indirect(entries(offs_sb, HALVES[0])))
         w1_codes = deal_codes("w1_codes", w1_codes_raw)
+        nc.vector.tensor_copy(xq_codes[:, HALVES[0]], x_codes[:].indirect(entries(offs_sb, HALVES[0])))
         nc.vector.tensor_copy(xq_codes[:, HALVES[1]], x_codes[:].indirect(entries(offs_sb, HALVES[1])))
+        w1_plane = deal_plane("w1_plane", w1_plane_raw, [slice(0, 1), slice(1, PACK)])
 
         y_win = [sb("y_win%d" % t, [P, S if t == 0 else 2 * S], F32) for t in range(PACK)]
         y_last = sb("y_last", [P, S], F32)
@@ -128,9 +129,9 @@ def tile_picked_skippullbfrac_none_po_kernel(
             nc.scalar.copy(y_flat[t][:, cols], y_ps[:])
 
         w2_codes = deal_codes("w2_codes", w2_codes_raw)
-        w2_plane = deal_plane("w2_plane", w2_plane_raw)
+        w2_plane = deal_plane("w2_plane", w2_plane_raw, [slice(0, PACK)])
         gain2 = sb("gain2", [P, PACK], F32)
-        nc.vector.tensor_scalar(gain2[:], gain[:], -2.0, None, ALU.mult)
+        nc.gpsimd.tensor_scalar(gain2[:], gain[:], -2.0, 0.0, ALU.mult, ALU.add)
 
         d1 = sb("d1", [P, PACK, S], F32)
         d2 = sb("d2", [P, PACK, S], F32)
@@ -167,7 +168,8 @@ def tile_picked_skippullbfrac_none_po_kernel(
                     ALU.mult,
                 )
         gate = logs
-        h_win = [sb("h_win%d" % t, [P, S], F32) for t in range(PACK)]
+        h_last = sb("h_last", [P, S], F32)
+        h_win = y_win[1:] + [h_last]
         h_ps = {}
 
         def gate_of(t, d4):
@@ -187,25 +189,20 @@ def tile_picked_skippullbfrac_none_po_kernel(
         second_layer(0, HALVES[0])
         diff(d1[:, 3, :], 1, n4_sb)
         second_layer(1, HALVES[1])
-        diff(d1[:, 2, :], 2, n4_sb)
-        diff(d1[:, 1, :], 3, n4_sb)
-        d4 = [d4_first[:], d1[:, 3, :], d1[:, 2, :], d1[:, 1, :]]
+        d4_late = [sb("d4_late%d" % u, [P, S], F32, tag="z_grouped%d" % u) for u in range(2)]
+        for u in range(2):
+            diff(d4_late[u][:], 2 + u, n4_sb)
+        d4 = [d4_first[:], d1[:, 3, :], d4_late[0][:], d4_late[1][:]]
         for t in range(PACK):
             gate_of(t, d4[t])
             for u, cols in enumerate(HALVES):
                 nc.scalar.copy(h_win[t][:, cols], h_ps[t // 2, u][:, HALVES[t % 2]])
 
-        pulled = sb("pulled", [P, PACK, S], F32)
         kept = sb("kept", [P, PACK, S], F32)
-        res = sb("res", [P, PACK, S], F32)
-        res_grouped = sb("res_grouped", [P, S, PACK], BF16)
         res_codes = sb("res_codes", [P, S], U32)
         res_plane = sb("res_plane", [P, S], U8)
         out_rows = out_0.rearrange("(p t) j -> p t j", t=PACK)
         out_words = packed_rows(out_1)
-
-        def pull(t, cols):
-            nc.vector.tensor_tensor(pulled[:, t, cols], h_win[t][:].indirect(entries(n3_sb, cols)), gate[:, t, cols], ALU.mult)
 
         def keep_own(pair, u):
             rows = slice(2 * pair, 2 * pair + 2)
@@ -214,41 +211,46 @@ def tile_picked_skippullbfrac_none_po_kernel(
                 kept[:, rows, HALVES[u]], gate[:, rows, HALVES[u]], 1.0, h_pair, ALU.subtract, ALU.mult
             )
 
-        def finish(cols):
-            nc.vector.tensor_tensor(res[:, :, cols], pulled[:, :, cols], kept[:, :, cols], ALU.subtract)
-            nc.sync.dma_start(out=out_rows[:, :, cols], in_=res[:, :, cols])
+        pulled = sb("pulled", [P, PACK, S], F32)
+
+        def pull(t, cols):
+            nc.vector.tensor_tensor(pulled[:, t, cols], h_win[t][:].indirect(entries(n3_sb, cols)), gate[:, t, cols], ALU.mult)
+
+        res = sb("res", [P, PACK, S], F32)
+        grouped = sb("grouped", [P, S, PACK], BF16)
+
+        def finish(rows, cols):
+            nc.vector.tensor_tensor(res[:, rows, cols], pulled[:, rows, cols], kept[:, rows, cols], ALU.subtract)
+            nc.sync.dma_start(out=out_rows[:, rows, cols], in_=res[:, rows, cols])
 
         def regroup(copy, cols):
-            copy(res_grouped[:, cols, :], res[:, :, cols].rearrange("p t j -> p j t"))
+            copy(grouped[:, cols, :], res[:, :, cols].rearrange("p t j -> p j t"))
 
         def hand_on(cols):
             nc.vector.quantize_mx(
                 out=res_codes[:, cols].bitcast(FP8X4),
                 scales=res_plane[:, cols],
-                in_=res_grouped[:, cols, :].rearrange("p j t -> p (j t)"),
+                in_=grouped[:, cols, :].rearrange("p j t -> p (j t)"),
             )
             nc.sync.dma_start(out=out_words[:, cols], in_=res_codes[:, cols].bitcast(I32))
 
-        pieces = (slice(0, HALF), slice(HALF, HALF + 128), slice(HALF + 128, S))
-        for t in range(PACK):
-            if t % 2 == 0:
-                keep_own(t // 2, 0)
-            pull(t, pieces[0])
-        keep_own(0, 1)
-        finish(pieces[0])
-        regroup(nc.scalar.copy, pieces[0])
-        keep_own(1, 1)
-        for t in range(PACK):
-            pull(t, pieces[1])
-        hand_on(pieces[0])
-        finish(pieces[1])
-        regroup(nc.scalar.copy, pieces[1])
-        for t in range(PACK):
-            pull(t, pieces[2])
-        hand_on(pieces[1])
-        finish(pieces[2])
-        regroup(nc.vector.tensor_copy, pieces[2])
-        hand_on(pieces[2])
+        first, second = HALVES
+        low, high = slice(0, 2), slice(2, PACK)
+        for u in range(2):
+            for pair in range(2):
+                keep_own(pair, u)
+        for t in range(PACK - 1):
+            pull(t, WHOLE)
+        pull(PACK - 1, first)
+        finish(low, first)
+        pull(PACK - 1, second)
+        finish(high, first)
+        regroup(nc.scalar.copy, first)
+        finish(slice(0, PACK), second)
+        regroup(nc.scalar.copy, slice(HALF, HALF + 64))
+        regroup(nc.vector.tensor_copy, slice(HALF + 64, S))
+        hand_on(first)
+        hand_on(second)
         for q in range(4):
             engine = nc.sync if q % 2 == 0 else nc.scalar
             engine.dma_start(out=out_2[0, 4 * q : 4 * q + 4, :].bitcast(I32), in_=res_plane[32 * q : 32 * q + 4, :].bitcast(I32))

@@ -20,7 +20,6 @@ PACK = 4
 HALF = S // 2
 HALVES = (slice(0, HALF), slice(HALF, S))
 WHOLE = slice(0, S)
-TINY = 2.0 ** -60
 
 
 def load_scale_rows(engine, plane, scales, quadrants=range(4)):
@@ -75,14 +74,14 @@ def tile_picked_skippullbfrac_none_po_kernel(
         w2_codes_raw = sb("w2_codes_raw", [P, N], I32)
         w2_plane_raw = sb("w2_plane_raw", [P, N], U8)
         gain = sb("gain", [P, PACK], F32)
-        tiny = sb("tiny", [P, 1], F32)
+        half = sb("half", [P, 1], F32)
         warm = sb("warm", [P, 1], F32)
 
         nc.gpsimd.memset(w1_plane_raw[:].bitcast(I32), 0)
         nc.vector.memset(x_plane[:].bitcast(I32), 0)
-        nc.vector.memset(tiny[:], TINY)
+        nc.vector.memset(half[:], 0.5)
         nc.vector.memset(w2_plane_raw[:].bitcast(I32), 0)
-        nc.scalar.activation(warm[:], tiny[:], ACT.Ln)
+        nc.scalar.activation(warm[:], half[:], ACT.Abs_reciprocal_sqrt)
 
         nc.sync.dma_start(offs_sb[:], offs)
         nc.sync.dma_start(out=x_codes[:, : T // 2].bitcast(I32), in_=packed_rows(x_words)[:, : T // 2])
@@ -131,7 +130,7 @@ def tile_picked_skippullbfrac_none_po_kernel(
         w2_codes = deal_codes("w2_codes", w2_codes_raw)
         w2_plane = deal_plane("w2_plane", w2_plane_raw, [slice(0, PACK)])
         gain2 = sb("gain2", [P, PACK], F32)
-        nc.gpsimd.tensor_scalar(gain2[:], gain[:], -2.0, 0.0, ALU.mult, ALU.add)
+        nc.gpsimd.tensor_scalar(gain2[:], gain[:], -1.0, 0.0, ALU.mult, ALU.add)
 
         d1 = sb("d1", [P, PACK, S], F32)
         d2 = sb("d2", [P, PACK, S], F32)
@@ -145,27 +144,19 @@ def tile_picked_skippullbfrac_none_po_kernel(
         for t in range(PACK):
             diff(d2[:, t, :], t, n2_sb)
             nc.scalar.activation(mag[:, t, :], d2[:, t, :], ACT.Abs)
-            nc.scalar.activation(logs[:, t, :], mag[:, t, :], ACT.Ln, bias=tiny[:], scale=2.0)
+            nc.scalar.activation(logs[:, t, :], mag[:, t, :], ACT.Abs_reciprocal_sqrt, bias=half[:])
+            nc.scalar.activation(mag[:, t, :], logs[:, t, :], ACT.Square)
         for t in range(PACK):
             diff(d1[:, t, :], t, n1_sb)
-        d4_first = sb("d4_first", [P, S], F32)
-        diff(d4_first[:], 0, n4_sb)
 
-        recip = mag[:].rearrange("p c (u t i) -> p u t c i", u=2, t=PACK)
         z_planes = sb("z_planes", [P, PACK, S], BF16)
         z_grouped = [sb("z_grouped%d" % u, [P, HALF, PACK], BF16) for u in range(2)]
         z_codes = sb("z_codes", [P, S], U32)
         z_plane = sb("z_plane", [P, S], U8)
         for u, cols in enumerate(HALVES):
             for t in range(PACK):
-                nc.scalar.activation(recip[:, u, t], logs[:, t, cols].rearrange("p (c i) -> p c i", c=PACK), ACT.Sigmoid, scale=-1.0)
                 nc.vector.scalar_tensor_tensor(
-                    z_planes[:, t, cols].rearrange("p (c i) -> p c i", c=PACK),
-                    d1[:, t, cols].rearrange("p (c i) -> p c i", c=PACK),
-                    gain2[:, t : t + 1],
-                    recip[:, u, t],
-                    ALU.mult,
-                    ALU.mult,
+                    z_planes[:, t, cols], d1[:, t, cols], gain2[:, t : t + 1], mag[:, t, cols], ALU.mult, ALU.mult
                 )
         gate = logs
         h_last = sb("h_last", [P, S], F32)
@@ -186,13 +177,15 @@ def tile_picked_skippullbfrac_none_po_kernel(
 
         for u, cols in enumerate(HALVES):
             nc.scalar.copy(z_grouped[u][:], z_planes[:, :, cols].rearrange("p t j -> p j t"))
+        diff(d1[:, 3, :], 0, n4_sb)
         second_layer(0, HALVES[0])
-        diff(d1[:, 3, :], 1, n4_sb)
+        d4_mid = sb("d4_mid", [P, S], F32, tag="z_grouped0")
+        diff(d4_mid[:], 1, n4_sb)
         second_layer(1, HALVES[1])
-        d4_late = [sb("d4_late%d" % u, [P, S], F32, tag="z_grouped%d" % u) for u in range(2)]
+        d4_late = sb("d4_late", [P, 2, S], F32, tag="z_grouped1")
         for u in range(2):
-            diff(d4_late[u][:], 2 + u, n4_sb)
-        d4 = [d4_first[:], d1[:, 3, :], d4_late[0][:], d4_late[1][:]]
+            diff(d4_late[:, u, :], 2 + u, n4_sb)
+        d4 = [d1[:, 3, :], d4_mid[:], d4_late[:, 0, :], d4_late[:, 1, :]]
         for t in range(PACK):
             gate_of(t, d4[t])
             for u, cols in enumerate(HALVES):

@@ -20,6 +20,7 @@ PACK = 4
 HALF = S // 2
 HALVES = (slice(0, HALF), slice(HALF, S))
 WHOLE = slice(0, S)
+TINY = 2.0 ** -100
 
 
 def load_scale_rows(engine, plane, scales, quadrants=range(4)):
@@ -76,26 +77,28 @@ def tile_picked_skippullbfrac_none_po_kernel(
         gain = sb("gain", [P, PACK], F32)
         half = sb("half", [P, 1], F32)
         warm = sb("warm", [P, 1], F32)
+        tiny = sb("tiny", [P, 1], F32)
 
+        nc.gpsimd.memset(x_plane[:, : T // 2].bitcast(I32), 0)
+        nc.vector.memset(x_plane[:, T // 2 :].bitcast(I32), 0)
         nc.gpsimd.memset(w1_plane_raw[:].bitcast(I32), 0)
-        nc.vector.memset(x_plane[:].bitcast(I32), 0)
         nc.vector.memset(half[:], 0.5)
+        nc.vector.memset(tiny[:], TINY)
         nc.vector.memset(w2_plane_raw[:].bitcast(I32), 0)
         nc.scalar.activation(warm[:], half[:], ACT.Abs_reciprocal_sqrt)
 
         nc.sync.dma_start(offs_sb[:], offs)
-        nc.sync.dma_start(out=x_codes[:, : T // 2].bitcast(I32), in_=packed_rows(x_words)[:, : T // 2])
-        load_scale_rows(nc.sync, x_plane, x_scales)
         nc.sync.dma_start(out=w1_codes_raw[:], in_=packed_rows(w1_words))
-        nc.sync.dma_start(out=x_codes[:, T // 2 :].bitcast(I32), in_=packed_rows(x_words)[:, T // 2 :])
-        load_scale_rows(nc.sync, w1_plane_raw, w1_scales, range(0, 1))
-        load_scale_rows(nc.gpsimd, w1_plane_raw, w1_scales, range(1, 4))
+        load_scale_rows(nc.sync, x_plane, x_scales)
+        nc.sync.dma_start(out=x_codes[:].bitcast(I32), in_=packed_rows(x_words))
+        load_scale_rows(nc.sync, w1_plane_raw, w1_scales, range(0, 2))
+        load_scale_rows(nc.gpsimd, w1_plane_raw, w1_scales, range(2, 4))
+        nc.sync.dma_start(out=gain[:], in_=gn.rearrange("(p t) o -> p (t o)", t=PACK))
         nc.sync.dma_start(n2_sb[:], n2)
         nc.sync.dma_start(out=w2_codes_raw[:], in_=packed_rows(w2_words))
         load_scale_rows(nc.sync, w2_plane_raw, w2_scales)
         nc.sync.dma_start(n1_sb[:], n1)
         nc.sync.dma_start(n4_sb[:], n4)
-        nc.sync.dma_start(out=gain[:], in_=gn.rearrange("(p t) o -> p (t o)", t=PACK))
         nc.sync.dma_start(n3_sb[:], n3)
 
         def deal_codes(name, raw):
@@ -117,6 +120,17 @@ def tile_picked_skippullbfrac_none_po_kernel(
         nc.vector.tensor_copy(xq_codes[:, HALVES[1]], x_codes[:].indirect(entries(offs_sb, HALVES[1])))
         w1_plane = deal_plane("w1_plane", w1_plane_raw, [slice(0, 1), slice(1, PACK)])
 
+        gain_sign = sb("gain_sign", [P, PACK], F32)
+        flip = sb("flip", [P, PACK], F32)
+        gain_size = sb("gain_size", [P, PACK], F32)
+        gain_rsqrt = sb("gain_rsqrt", [P, PACK], F32)
+        gain_root = sb("gain_root", [P, PACK], F32)
+        nc.scalar.activation(gain_sign[:], gain[:], ACT.Sign)
+        nc.scalar.activation(flip[:], gain_sign[:], ACT.Sign, bias=half[:], scale=-1.0)
+        nc.scalar.activation(gain_size[:], gain[:], ACT.Abs)
+        nc.scalar.activation(gain_rsqrt[:], gain_size[:], ACT.Abs_reciprocal_sqrt, bias=tiny[:])
+        nc.gpsimd.tensor_tensor(gain_root[:], gain_size[:], gain_rsqrt[:], ALU.mult)
+
         y_win = [sb("y_win%d" % t, [P, S if t == 0 else 2 * S], F32) for t in range(PACK)]
         y_last = sb("y_last", [P, S], F32)
         y_flat = [y_win[t + 1][:, S:] for t in range(PACK - 1)] + [y_last[:]]
@@ -124,13 +138,11 @@ def tile_picked_skippullbfrac_none_po_kernel(
         for number, (t, cols) in enumerate(y_pieces):
             y_ps = bank("y_ps%d" % number, number, cols.stop - cols.start)
             product(y_ps[:], w1_codes, w1_plane, t, xq_codes[:, cols], xq_plane[:, cols])
-            nc.scalar.copy(y_win[t][:, cols], y_ps[:])
-            nc.scalar.copy(y_flat[t][:, cols], y_ps[:])
+            nc.scalar.activation(y_win[t][:, cols], y_ps[:], ACT.Copy, scale=flip[:, t : t + 1])
+            nc.scalar.activation(y_flat[t][:, cols], y_ps[:], ACT.Copy, scale=flip[:, t : t + 1])
 
         w2_codes = deal_codes("w2_codes", w2_codes_raw)
         w2_plane = deal_plane("w2_plane", w2_plane_raw, [slice(0, PACK)])
-        gain2 = sb("gain2", [P, PACK], F32)
-        nc.gpsimd.tensor_scalar(gain2[:], gain[:], -1.0, 0.0, ALU.mult, ALU.add)
 
         d1 = sb("d1", [P, PACK, S], F32)
         d2 = sb("d2", [P, PACK, S], F32)
@@ -145,7 +157,7 @@ def tile_picked_skippullbfrac_none_po_kernel(
             diff(d2[:, t, :], t, n2_sb)
             nc.scalar.activation(mag[:, t, :], d2[:, t, :], ACT.Abs)
             nc.scalar.activation(logs[:, t, :], mag[:, t, :], ACT.Abs_reciprocal_sqrt, bias=half[:])
-            nc.scalar.activation(mag[:, t, :], logs[:, t, :], ACT.Square)
+            nc.scalar.activation(mag[:, t, :], logs[:, t, :], ACT.Square, scale=gain_root[:, t : t + 1])
         for t in range(PACK):
             diff(d1[:, t, :], t, n1_sb)
 
@@ -153,18 +165,16 @@ def tile_picked_skippullbfrac_none_po_kernel(
         z_grouped = [sb("z_grouped%d" % u, [P, HALF, PACK], BF16) for u in range(2)]
         z_codes = sb("z_codes", [P, S], U32)
         z_plane = sb("z_plane", [P, S], U8)
-        for u, cols in enumerate(HALVES):
-            for t in range(PACK):
-                nc.vector.scalar_tensor_tensor(
-                    z_planes[:, t, cols], d1[:, t, cols], gain2[:, t : t + 1], mag[:, t, cols], ALU.mult, ALU.mult
-                )
+        low, high = slice(0, 2), slice(2, PACK)
+        for rows, cols in ((low, WHOLE), (high, HALVES[0]), (high, HALVES[1])):
+            nc.vector.tensor_tensor(z_planes[:, rows, cols], d1[:, rows, cols], mag[:, rows, cols], ALU.mult)
         gate = logs
         h_last = sb("h_last", [P, S], F32)
         h_win = y_win[1:] + [h_last]
         h_ps = {}
 
         def gate_of(t, d4):
-            nc.scalar.activation(gate[:, t, :], d4, ACT.Sigmoid)
+            nc.scalar.activation(gate[:, t, :], d4, ACT.Sigmoid, scale=flip[:, t : t + 1])
 
         def second_layer(u, cols):
             nc.vector.quantize_mx(

from contextlib import ExitStack

import concourse.mybir as mybir

K, T, S, N, H = 512, 2048, 512, 512, 512
FLOPS = 2 * K * H * S + 2 * H * N * S

F32 = mybir.dt.float32
BF16 = mybir.dt.bfloat16
I32 = mybir.dt.int32
U32 = mybir.dt.uint32
U16 = mybir.dt.uint16
U8 = mybir.dt.uint8
FP8X4 = mybir.dt.float8_e4m3fn_x4
ALU = mybir.AluOpType
ACT = mybir.ActivationFunctionType

P = 128
PACK = 4
HALF = S // 2
HALVES = (slice(0, HALF), slice(HALF, S))
WHOLE = slice(0, S)
TINY = 2.0 ** -100


def load_scale_rows(engine, plane, scales, quadrants=range(4)):
    for q in quadrants:
        engine.dma_start(out=plane[32 * q : 32 * q + 4, :].bitcast(I32), in_=scales[0, 4 * q : 4 * q + 4, :].bitcast(I32))


def packed_rows(words):
    return words[0].rearrange("p n t -> p (n t)").bitcast(I32)


def entries(places, cols):
    return places[:, cols.start // 16 : cols.stop // 16]


def tile_picked_skippullbfrac_none_po_kernel(
    tc, x_words, x_scales, w1_words, w1_scales, gn, w2_words, w2_scales, offs, n1, n2, n3, n4, out_0, out_1, out_2
):
    nc = tc.nc
    with ExitStack() as ctx:
        lists = ctx.enter_context(tc.tile_pool(name="lists", bufs=1))
        keep = ctx.enter_context(tc.tile_pool(name="keep", bufs=1))
        psum = ctx.enter_context(tc.psum_pool(name="psum", bufs=1))

        def sb(name, shape, dtype, tag=None):
            return keep.tile(shape, dtype, name=name, tag=tag or name, align_bytes=64)

        def bank(name, number, width):
            return psum.tile([P, width], F32, name=name, tag="bank%d" % number)

        def product(out, codes, plane, t, rhs_codes, rhs_plane):
            nc.tensor.matmul_mx(
                out=out,
                lhsT=codes[:, t, :].bitcast(FP8X4),
                lhsT_scale=plane[:, t, :],
                rhs=rhs_codes.bitcast(FP8X4),
                rhs_scale=rhs_plane,
                start=True,
                stop=True,
            )

        offs_sb = lists.tile([P, S // 16], U16, name="offs_sb")
        n1_sb = lists.tile([P, S // 16], U16, name="n1_sb")
        n2_sb = lists.tile([P, S // 16], U16, name="n2_sb")
        n3_sb = lists.tile([P, S // 16], U16, name="n3_sb")
        n4_sb = lists.tile([P, S // 16], U16, name="n4_sb")

        x_codes = sb("x_codes", [P, T], U32)
        x_plane = sb("x_plane", [P, T], U8)
        w1_codes_raw = sb("w1_codes_raw", [P, H], I32)
        w1_plane_raw = sb("w1_plane_raw", [P, H], U8)
        w2_codes_raw = sb("w2_codes_raw", [P, N], I32)
        w2_plane_raw = sb("w2_plane_raw", [P, N], U8)
        gain = sb("gain", [P, PACK], F32)
        half = sb("half", [P, 1], F32)
        warm = sb("warm", [P, 1], F32)
        tiny = sb("tiny", [P, 1], F32)

        nc.gpsimd.memset(x_plane[:, : T // 2].bitcast(I32), 0)
        nc.vector.memset(x_plane[:, T // 2 :].bitcast(I32), 0)
        nc.gpsimd.memset(w1_plane_raw[:].bitcast(I32), 0)
        nc.vector.memset(half[:], 0.5)
        nc.vector.memset(tiny[:], TINY)
        nc.vector.memset(w2_plane_raw[:].bitcast(I32), 0)
        nc.scalar.activation(warm[:], half[:], ACT.Abs_reciprocal_sqrt)

        nc.sync.dma_start(offs_sb[:], offs)
        nc.sync.dma_start(out=w1_codes_raw[:], in_=packed_rows(w1_words))
        load_scale_rows(nc.sync, x_plane, x_scales)
        nc.sync.dma_start(out=x_codes[:].bitcast(I32), in_=packed_rows(x_words))
        load_scale_rows(nc.sync, w1_plane_raw, w1_scales, range(0, 2))
        load_scale_rows(nc.gpsimd, w1_plane_raw, w1_scales, range(2, 4))
        nc.sync.dma_start(out=gain[:], in_=gn.rearrange("(p t) o -> p (t o)", t=PACK))
        nc.sync.dma_start(n2_sb[:], n2)
        nc.sync.dma_start(out=w2_codes_raw[:], in_=packed_rows(w2_words))
        load_scale_rows(nc.sync, w2_plane_raw, w2_scales)
        nc.sync.dma_start(n1_sb[:], n1)
        nc.sync.dma_start(n4_sb[:], n4)
        nc.sync.dma_start(n3_sb[:], n3)

        def deal_codes(name, raw):
            codes = sb(name, [P, PACK, P], I32)
            nc.vector.tensor_copy(out=codes[:], in_=raw[:].rearrange("p (m t) -> p t m", t=PACK))
            return codes

        def deal_plane(name, raw, steps):
            plane = sb(name, [P, PACK, P], U8)
            for rows in steps:
                nc.vector.tensor_copy(out=plane[:, rows, :], in_=raw[:].rearrange("p (m t) -> p t m", t=PACK)[:, rows, :])
            return plane

        xq_plane = sb("xq_plane", [P, S], U8)
        xq_codes = sb("xq_codes", [P, S], U32)
        nc.vector.tensor_copy(xq_plane[:], x_plane[:].indirect(offs_sb[:]))
        w1_codes = deal_codes("w1_codes", w1_codes_raw)
        nc.vector.tensor_copy(xq_codes[:, HALVES[0]], x_codes[:].indirect(entries(offs_sb, HALVES[0])))
        nc.vector.tensor_copy(xq_codes[:, HALVES[1]], x_codes[:].indirect(entries(offs_sb, HALVES[1])))
        w1_plane = deal_plane("w1_plane", w1_plane_raw, [slice(0, 1), slice(1, PACK)])

        gain_sign = sb("gain_sign", [P, PACK], F32)
        flip = sb("flip", [P, PACK], F32)
        gain_size = sb("gain_size", [P, PACK], F32)
        gain_rsqrt = sb("gain_rsqrt", [P, PACK], F32)
        gain_root = sb("gain_root", [P, PACK], F32)
        nc.scalar.activation(gain_sign[:], gain[:], ACT.Sign)
        nc.scalar.activation(flip[:], gain_sign[:], ACT.Sign, bias=half[:], scale=-1.0)
        nc.scalar.activation(gain_size[:], gain[:], ACT.Abs)
        nc.scalar.activation(gain_rsqrt[:], gain_size[:], ACT.Abs_reciprocal_sqrt, bias=tiny[:])
        nc.gpsimd.tensor_tensor(gain_root[:], gain_size[:], gain_rsqrt[:], ALU.mult)

        y_win = [sb("y_win%d" % t, [P, S if t == 0 else 2 * S], F32) for t in range(PACK)]
        y_last = sb("y_last", [P, S], F32)
        y_flat = [y_win[t + 1][:, S:] for t in range(PACK - 1)] + [y_last[:]]
        y_pieces = [(0, HALVES[0]), (0, HALVES[1])] + [(t, WHOLE) for t in range(1, PACK)]
        for number, (t, cols) in enumerate(y_pieces):
            y_ps = bank("y_ps%d" % number, number, cols.stop - cols.start)
            product(y_ps[:], w1_codes, w1_plane, t, xq_codes[:, cols], xq_plane[:, cols])
            nc.scalar.activation(y_win[t][:, cols], y_ps[:], ACT.Copy, scale=flip[:, t : t + 1])
            nc.scalar.activation(y_flat[t][:, cols], y_ps[:], ACT.Copy, scale=flip[:, t : t + 1])

        w2_codes = deal_codes("w2_codes", w2_codes_raw)
        w2_plane = deal_plane("w2_plane", w2_plane_raw, [slice(0, PACK)])

        d1 = sb("d1", [P, PACK, S], F32)
        d2 = sb("d2", [P, PACK, S], F32)
        mag = sb("mag", [P, PACK, S], F32)
        logs = sb("logs", [P, PACK, S], F32)

        def diff(dst, t, places):
            for cols in HALVES if t == 0 else (WHOLE,):
                nc.vector.tensor_tensor(dst[:, cols], y_win[t][:].indirect(entries(places, cols)), y_flat[t][:, cols], ALU.subtract)

        for t in range(PACK):
            diff(d2[:, t, :], t, n2_sb)
            nc.scalar.activation(mag[:, t, :], d2[:, t, :], ACT.Abs)
            nc.scalar.activation(logs[:, t, :], mag[:, t, :], ACT.Abs_reciprocal_sqrt, bias=half[:])
            nc.scalar.activation(mag[:, t, :], logs[:, t, :], ACT.Square, scale=gain_root[:, t : t + 1])
        for t in range(PACK):
            diff(d1[:, t, :], t, n1_sb)

        z_planes = sb("z_planes", [P, PACK, S], BF16)
        z_grouped = [sb("z_grouped%d" % u, [P, HALF, PACK], BF16) for u in range(2)]
        z_codes = sb("z_codes", [P, S], U32)
        z_plane = sb("z_plane", [P, S], U8)
        low, high = slice(0, 2), slice(2, PACK)
        for rows, cols in ((low, WHOLE), (high, HALVES[0]), (high, HALVES[1])):
            nc.vector.tensor_tensor(z_planes[:, rows, cols], d1[:, rows, cols], mag[:, rows, cols], ALU.mult)
        gate = logs
        h_last = sb("h_last", [P, S], F32)
        h_win = y_win[1:] + [h_last]
        h_ps = {}

        def gate_of(t, d4):
            nc.scalar.activation(gate[:, t, :], d4, ACT.Sigmoid, scale=flip[:, t : t + 1])

        def second_layer(u, cols):
            nc.vector.quantize_mx(
                out=z_codes[:, cols].bitcast(FP8X4), scales=z_plane[:, cols], in_=z_grouped[u][:].rearrange("p j t -> p (j t)")
            )
            for pair in range(2):
                h_ps[pair, u] = bank("h_ps%d_%d" % (pair, u), PACK + 2 * u + pair, S)
                for e in range(2):
                    product(h_ps[pair, u][:, HALVES[e]], w2_codes, w2_plane, 2 * pair + e, z_codes[:, cols], z_plane[:, cols])

        for u, cols in enumerate(HALVES):
            nc.scalar.copy(z_grouped[u][:], z_planes[:, :, cols].rearrange("p t j -> p j t"))
        diff(d1[:, 3, :], 0, n4_sb)
        second_layer(0, HALVES[0])
        d4_mid = sb("d4_mid", [P, S], F32, tag="z_grouped0")
        diff(d4_mid[:], 1, n4_sb)
        second_layer(1, HALVES[1])
        d4_late = sb("d4_late", [P, 2, S], F32, tag="z_grouped1")
        for u in range(2):
            diff(d4_late[:, u, :], 2 + u, n4_sb)
        d4 = [d1[:, 3, :], d4_mid[:], d4_late[:, 0, :], d4_late[:, 1, :]]
        for t in range(PACK):
            gate_of(t, d4[t])
            for u, cols in enumerate(HALVES):
                nc.scalar.copy(h_win[t][:, cols], h_ps[t // 2, u][:, HALVES[t % 2]])

        kept = sb("kept", [P, PACK, S], F32)
        res_codes = sb("res_codes", [P, S], U32)
        res_plane = sb("res_plane", [P, S], U8)
        out_rows = out_0.rearrange("(p t) j -> p t j", t=PACK)
        out_words = packed_rows(out_1)

        def keep_own(pair, u):
            rows = slice(2 * pair, 2 * pair + 2)
            h_pair = h_ps[pair, u][:].rearrange("p (e j) -> p e j", e=2)
            nc.vector.scalar_tensor_tensor(
                kept[:, rows, HALVES[u]], gate[:, rows, HALVES[u]], 1.0, h_pair, ALU.subtract, ALU.mult
            )

        pulled = sb("pulled", [P, PACK, S], F32)

        def pull(t, cols):
            nc.vector.tensor_tensor(pulled[:, t, cols], h_win[t][:].indirect(entries(n3_sb, cols)), gate[:, t, cols], ALU.mult)

        res = sb("res", [P, PACK, S], F32)
        grouped = sb("grouped", [P, S, PACK], BF16)

        def finish(rows, cols):
            nc.vector.tensor_tensor(res[:, rows, cols], pulled[:, rows, cols], kept[:, rows, cols], ALU.subtract)
            nc.sync.dma_start(out=out_rows[:, rows, cols], in_=res[:, rows, cols])

        def regroup(copy, cols):
            copy(grouped[:, cols, :], res[:, :, cols].rearrange("p t j -> p j t"))

        def hand_on(cols):
            nc.vector.quantize_mx(
                out=res_codes[:, cols].bitcast(FP8X4),
                scales=res_plane[:, cols],
                in_=grouped[:, cols, :].rearrange("p j t -> p (j t)"),
            )
            nc.sync.dma_start(out=out_words[:, cols], in_=res_codes[:, cols].bitcast(I32))

        first, second = HALVES
        low, high = slice(0, 2), slice(2, PACK)
        for u in range(2):
            for pair in range(2):
                keep_own(pair, u)
        for t in range(PACK - 1):
            pull(t, WHOLE)
        pull(PACK - 1, first)
        finish(low, first)
        pull(PACK - 1, second)
        finish(high, first)
        regroup(nc.scalar.copy, first)
        finish(slice(0, PACK), second)
        regroup(nc.scalar.copy, slice(HALF, HALF + 64))
        regroup(nc.vector.tensor_copy, slice(HALF + 64, S))
        hand_on(first)
        hand_on(second)
        for q in range(4):
            engine = nc.sync if q % 2 == 0 else nc.scalar
            engine.dma_start(out=out_2[0, 4 * q : 4 * q + 4, :].bitcast(I32), in_=res_plane[32 * q : 32 * q + 4, :].bitcast(I32))
